import numpy as np
import ml_dtypes

BF16 = ml_dtypes.bfloat16


def bf(x):
    return np.asarray(x, np.float32).astype(BF16)


def f32(x):
    return np.asarray(x, np.float32)


def f64(x):
    return np.asarray(x).astype(np.float64)


def striped(idx):
    return np.tile(idx.reshape(-1, 16).T, (8, 1))


S, K, M, N, E, Q = 512, 256, 128, 128, 2, 64


def setup_inputs():
    return {"base": bf(np.random.standard_normal((M, S))), "x": bf(np.random.standard_normal((K, N))), "w": bf(1.2 * np.random.standard_normal((E, K, M)) / np.sqrt(K)), "s": f32(0.5 + np.random.random_sample((M, 1))), "offs": striped(np.random.permutation(S)[:N])}


def reference(base, x, w, s, offs):
    idx = offs[:16].T.reshape(-1)
    z = f64(base).copy()
    for e in range(E):
        z[:, idx[e * Q : (e + 1) * Q]] += f64(w)[e].T @ f64(x)[:, e * Q : (e + 1) * Q]
    z = z / np.sqrt((z**2).mean(axis=0, keepdims=True) + 1e-5) * f64(s)
    return z

@@ -1,0 +1,68 @@
+import concourse.mybir as mybir
+from concourse.masks import make_identity
+
+P = 128
+S = 512
+K = 256
+N = 128
+E = 2
+Q = N // E
+A = K // P
+OFFSET_ROWS = 16
+EPS = 1e-5
+
+FLOPS = 2 * K * P * N + 4 * P * S
+
+BF16, F32, U16 = mybir.dt.bfloat16, mybir.dt.float32, mybir.dt.uint16
+mult = mybir.AluOpType.mult
+ACT = mybir.ActivationFunctionType
+
+
+def tile_rows_placenorm_base_kernel(tc, base, x, w, s, offs, out):
+    nc = tc.nc
+    with (
+        tc.tile_pool(name="held", bufs=1) as held,
+        tc.psum_pool(name="psum", bufs=1) as psum,
+    ):
+        offsets = held.tile([P, N // OFFSET_ROWS], U16)
+        base_t = held.tile([P, S], BF16)
+        x_t = held.tile([P, A * N], BF16)
+        w_t = held.tile([P, E, A * P], BF16)
+        gain = held.tile([P, 1], F32)
+
+        nc.sync.dma_start(base_t[:], base)
+        nc.sync.dma_start(x_t[:], x.rearrange("(p a) n -> p (a n)", a=A))
+        nc.sync.dma_start(w_t[:], w.rearrange("e (p a) m -> p e (a m)", a=A))
+        nc.sync.dma_start(offsets[:], offs)
+        nc.sync.dma_start(gain[:], s)
+
+        ident = held.tile([P, P], BF16)
+        make_identity(nc, ident[:])
+        eps = held.tile([P, 1], F32)
+        nc.vector.memset(eps[:], EPS)
+        averaging = held.tile([P, P], BF16)
+        nc.vector.memset(averaging[:], 1.0 / P)
+
+        window = psum.tile([P, S], F32)
+        nc.tensor.matmul(window[:], ident[:], base_t[:], start=True, stop=False)
+        piece = Q // OFFSET_ROWS
+        for e in range(E):
+            places = offsets[:, e * piece : (e + 1) * piece]
+            for a in range(A):
+                nc.tensor.matmul(
+                    window[:].indirect(places),
+                    w_t[:, e, a * P : (a + 1) * P],
+                    x_t[:, a * N + e * Q : a * N + (e + 1) * Q],
+                    start=False,
+                    stop=(e == E - 1 and a == A - 1),
+                )
+
+        squares = held.tile([P, S], BF16)
+        nc.scalar.activation(squares[:], window[:], ACT.Square)
+        mean_sq = psum.tile([P, S], F32)
+        nc.tensor.matmul(mean_sq[:], averaging[:], squares[:], start=True, stop=True)
+        rstd = held.tile([P, S], F32)
+        nc.scalar.activation(rstd[:], mean_sq[:], ACT.Abs_reciprocal_sqrt, bias=eps[:])
+        result = held.tile([P, S], F32)
+        nc.vector.scalar_tensor_tensor(result[:], window[:], gain[:], rstd[:], mult, mult)
+        nc.sync.dma_start(out, result[:])

@@ -10,6 +10,7 @@ Q = N // E
 A = K // P
 OFFSET_ROWS = 16
 EPS = 1e-5
+PART = S // 2
 
 FLOPS = 2 * K * P * N + 4 * P * S
 
@@ -22,7 +23,9 @@ def tile_rows_placenorm_base_kernel(tc, base, x, w, s, offs, out):
     nc = tc.nc
     with (
         tc.tile_pool(name="held", bufs=1) as held,
+        tc.tile_pool(name="work", bufs=S // PART) as work,
         tc.psum_pool(name="psum", bufs=1) as psum,
+        tc.psum_pool(name="mean_psum", bufs=S // PART) as mean_pool,
     ):
         offsets = held.tile([P, N // OFFSET_ROWS], U16)
         base_t = held.tile([P, S], BF16)
@@ -40,6 +43,8 @@ def tile_rows_placenorm_base_kernel(tc, base, x, w, s, offs, out):
         make_identity(nc, ident[:])
         eps = held.tile([P, 1], F32)
         nc.vector.memset(eps[:], EPS)
+        first_rsqrt = held.tile([P, 1], F32)
+        nc.scalar.activation(first_rsqrt[:], eps[:], ACT.Abs_reciprocal_sqrt)
         averaging = held.tile([P, P], BF16)
         nc.vector.memset(averaging[:], 1.0 / P)
 
@@ -57,12 +62,17 @@ def tile_rows_placenorm_base_kernel(tc, base, x, w, s, offs, out):
                     stop=(e == E - 1 and a == A - 1),
                 )
 
-        squares = held.tile([P, S], BF16)
-        nc.scalar.activation(squares[:], window[:], ACT.Square)
-        mean_sq = psum.tile([P, S], F32)
-        nc.tensor.matmul(mean_sq[:], averaging[:], squares[:], start=True, stop=True)
-        rstd = held.tile([P, S], F32)
-        nc.scalar.activation(rstd[:], mean_sq[:], ACT.Abs_reciprocal_sqrt, bias=eps[:])
-        result = held.tile([P, S], F32)
-        nc.vector.scalar_tensor_tensor(result[:], window[:], gain[:], rstd[:], mult, mult)
-        nc.sync.dma_start(out, result[:])
+        parts = [slice(c, c + PART) for c in range(0, S, PART)]
+        means = []
+        for cols in parts:
+            squares = work.tile([P, PART], BF16)
+            nc.scalar.activation(squares[:], window[:, cols], ACT.Square)
+            mean_sq = mean_pool.tile([P, PART], F32)
+            nc.tensor.matmul(mean_sq[:], averaging[:], squares[:], start=True, stop=True)
+            means.append(mean_sq)
+        for cols, mean_sq in zip(parts, means):
+            rstd = work.tile([P, PART], F32)
+            nc.scalar.activation(rstd[:], mean_sq[:], ACT.Abs_reciprocal_sqrt, bias=eps[:])
+            result = work.tile([P, PART], F32)
+            nc.vector.scalar_tensor_tensor(result[:], window[:, cols], gain[:], rstd[:], mult, mult)
+            nc.sync.dma_start(out[:, cols], result[:])

@@ -10,7 +10,8 @@ Q = N // E
 A = K // P
 OFFSET_ROWS = 16
 EPS = 1e-5
-PART = S // 2
+PART = S // 4
+WARM_UPS = 12
 
 FLOPS = 2 * K * P * N + 4 * P * S
 
@@ -39,14 +40,19 @@ def tile_rows_placenorm_base_kernel(tc, base, x, w, s, offs, out):
         nc.sync.dma_start(offsets[:], offs)
         nc.sync.dma_start(gain[:], s)
 
+        averaging = held.tile([P, P], BF16)
+        nc.vector.memset(averaging[:], 1.0 / P)
+
+        spare = psum.tile([P, P], F32)
+        for i in range(WARM_UPS):
+            nc.tensor.matmul(spare[:], averaging[:], averaging[:], start=True, stop=True)
+
         ident = held.tile([P, P], BF16)
         make_identity(nc, ident[:])
         eps = held.tile([P, 1], F32)
         nc.vector.memset(eps[:], EPS)
         first_rsqrt = held.tile([P, 1], F32)
         nc.scalar.activation(first_rsqrt[:], eps[:], ACT.Abs_reciprocal_sqrt)
-        averaging = held.tile([P, P], BF16)
-        nc.vector.memset(averaging[:], 1.0 / P)
 
         window = psum.tile([P, S], F32)
         nc.tensor.matmul(window[:], ident[:], base_t[:], start=True, stop=False)

@@ -35,10 +35,10 @@ def tile_rows_placenorm_base_kernel(tc, base, x, w, s, offs, out):
         gain = held.tile([P, 1], F32)
 
         nc.sync.dma_start(base_t[:], base)
-        nc.sync.dma_start(x_t[:], x.rearrange("(p a) n -> p (a n)", a=A))
-        nc.sync.dma_start(w_t[:], w.rearrange("e (p a) m -> p e (a m)", a=A))
         nc.sync.dma_start(offsets[:], offs)
-        nc.sync.dma_start(gain[:], s)
+        nc.scalar.dma_start(w_t[:], w.rearrange("e (p a) m -> p e (a m)", a=A))
+        nc.scalar.dma_start(x_t[:], x.rearrange("(p a) n -> p (a n)", a=A))
+        nc.scalar.dma_start(gain[:], s)
 
         averaging = held.tile([P, P], BF16)
         nc.vector.memset(averaging[:], 1.0 / P)

import concourse.mybir as mybir
from concourse.masks import make_identity

P = 128
S = 512
K = 256
N = 128
E = 2
Q = N // E
A = K // P
OFFSET_ROWS = 16
EPS = 1e-5
PART = S // 4
WARM_UPS = 12

FLOPS = 2 * K * P * N + 4 * P * S

BF16, F32, U16 = mybir.dt.bfloat16, mybir.dt.float32, mybir.dt.uint16
mult = mybir.AluOpType.mult
ACT = mybir.ActivationFunctionType


def tile_rows_placenorm_base_kernel(tc, base, x, w, s, offs, out):
    nc = tc.nc
    with (
        tc.tile_pool(name="held", bufs=1) as held,
        tc.tile_pool(name="work", bufs=S // PART) as work,
        tc.psum_pool(name="psum", bufs=1) as psum,
        tc.psum_pool(name="mean_psum", bufs=S // PART) as mean_pool,
    ):
        offsets = held.tile([P, N // OFFSET_ROWS], U16)
        base_t = held.tile([P, S], BF16)
        x_t = held.tile([P, A * N], BF16)
        w_t = held.tile([P, E, A * P], BF16)
        gain = held.tile([P, 1], F32)

        nc.sync.dma_start(base_t[:], base)
        nc.sync.dma_start(offsets[:], offs)
        nc.scalar.dma_start(w_t[:], w.rearrange("e (p a) m -> p e (a m)", a=A))
        nc.scalar.dma_start(x_t[:], x.rearrange("(p a) n -> p (a n)", a=A))
        nc.scalar.dma_start(gain[:], s)

        averaging = held.tile([P, P], BF16)
        nc.vector.memset(averaging[:], 1.0 / P)

        spare = psum.tile([P, P], F32)
        for i in range(WARM_UPS):
            nc.tensor.matmul(spare[:], averaging[:], averaging[:], start=True, stop=True)

        ident = held.tile([P, P], BF16)
        make_identity(nc, ident[:])
        eps = held.tile([P, 1], F32)
        nc.vector.memset(eps[:], EPS)
        first_rsqrt = held.tile([P, 1], F32)
        nc.scalar.activation(first_rsqrt[:], eps[:], ACT.Abs_reciprocal_sqrt)

        window = psum.tile([P, S], F32)
        nc.tensor.matmul(window[:], ident[:], base_t[:], start=True, stop=False)
        piece = Q // OFFSET_ROWS
        for e in range(E):
            places = offsets[:, e * piece : (e + 1) * piece]
            for a in range(A):
                nc.tensor.matmul(
                    window[:].indirect(places),
                    w_t[:, e, a * P : (a + 1) * P],
                    x_t[:, a * N + e * Q : a * N + (e + 1) * Q],
                    start=False,
                    stop=(e == E - 1 and a == A - 1),
                )

        parts = [slice(c, c + PART) for c in range(0, S, PART)]
        means = []
        for cols in parts:
            squares = work.tile([P, PART], BF16)
            nc.scalar.activation(squares[:], window[:, cols], ACT.Square)
            mean_sq = mean_pool.tile([P, PART], F32)
            nc.tensor.matmul(mean_sq[:], averaging[:], squares[:], start=True, stop=True)
            means.append(mean_sq)
        for cols, mean_sq in zip(parts, means):
            rstd = work.tile([P, PART], F32)
            nc.scalar.activation(rstd[:], mean_sq[:], ACT.Abs_reciprocal_sqrt, bias=eps[:])
            result = work.tile([P, PART], F32)
            nc.vector.scalar_tensor_tensor(result[:], window[:, cols], gain[:], rstd[:], mult, mult)
            nc.sync.dma_start(out[:, cols], result[:])
